import numpy as np
import ml_dtypes


def mxq(x, axis, fmt="e4m3"):
    dtype, down = {"e4m3": (ml_dtypes.float8_e4m3fn, 7), "e5m2": (ml_dtypes.float8_e5m2, 14)}[fmt]
    v = np.moveaxis(np.asarray(x, np.float32).astype(ml_dtypes.bfloat16).astype(np.float64), axis, -1)
    blocks = v.reshape(v.shape[:-1] + (-1, 32))
    amax = np.abs(blocks).max(-1, keepdims=True)
    byte = np.maximum(np.where(amax > 0, np.frexp(amax)[1] - 1 + 127, 0) - down, 1)
    scale = np.exp2(byte - 127.0)
    codes = (blocks / scale).astype(np.float32).astype(dtype).astype(np.float64)
    return np.moveaxis((codes * scale).reshape(v.shape), -1, axis)


WIDE = False


def mx_kscale(k):
    if not WIDE:
        return np.ones(k)
    levels = np.array([30, -30])
    if k % 512:
        return np.exp2(np.random.permutation(np.resize(levels, k // 32))).repeat(32)
    a = np.empty((k // 512, 16))
    for p in range(k // 512):
        a[p, :8] = np.random.permutation(np.resize(levels, 8))
        for g in range(8):
            far = levels[np.abs(levels - a[p, g]) >= 10]
            a[p, g + 8] = far[np.random.randint(len(far))]
    return np.exp2(a.ravel()).repeat(32)


def f64(x):
    return np.asarray(x).astype(np.float64)


def striped(idx):
    return np.tile(np.asarray(idx).reshape(-1, 16).T, (8, 1)).astype(np.uint16)


def unstriped(offs):
    return offs[:16].T.reshape(-1).astype(np.int64)


E2M1 = np.array([0.0, 0.5, 1.0, 1.5, 2.0, 3.0, 4.0, 6.0, -0.0, -0.5, -1.0, -1.5, -2.0, -3.0, -4.0, -6.0])


def pack_weight(w, fmt):
    k, n = w.shape
    w = f64(np.asarray(w, np.float32).astype(ml_dtypes.bfloat16)).reshape(k // 32, 32, n)
    amax = np.abs(w).max(1)
    if fmt == "e4m3":
        byte = np.frexp(amax)[1] - 1 + 127 - 7
    else:
        mant, ex = np.frexp(amax / 6.0)
        byte = np.where(mant > 0.5, ex, ex - 1) + 127
    byte = np.clip(np.where(amax > 0, byte, 1), 1, 254)
    scaled = (w * np.exp2(127.0 - byte)[:, None, :]).reshape(k, n).astype(np.float32)
    by_word = np.ascontiguousarray(scaled.reshape(k // 512, 128, 4, n).transpose(0, 1, 3, 2))
    if fmt == "e4m3":
        words = by_word.astype(ml_dtypes.float8_e4m3fn).view(np.uint8)
    else:
        c = by_word.astype(ml_dtypes.float4_e2m1fn).view(np.uint8) & 0xF
        words = (c[..., 0::2] | (c[..., 1::2] << 4)).reshape(k // 512, 128, 2 * n)
    return np.ascontiguousarray(words), np.ascontiguousarray(byte.astype(np.uint8).reshape(k // 512, 16, n))


def unpack_weight(words, scales, fmt):
    g, _, n = scales.shape
    words = np.ascontiguousarray(words).reshape(g, 128, n, -1)
    if fmt == "e4m3":
        vals = words.view(ml_dtypes.float8_e4m3fn).astype(np.float64)
    else:
        nib = np.empty((g, 128, n, 4), np.uint8)
        nib[..., 0::2] = words & 0xF
        nib[..., 1::2] = words >> 4
        vals = E2M1[nib]
    vals = vals * np.repeat(np.exp2(scales.astype(np.float64) - 127.0), 8, axis=1)[..., None]
    return vals.transpose(0, 1, 3, 2).reshape(g * 512, n)


K, T, J, R, C, O, N, E = 512, 1024, 256, 512, 512, 256, 256, 128


def setup_inputs():
    n = np.random.standard_normal
    idx = np.random.permutation(T)[:J]
    idx2 = np.random.permutation(C)[:J]
    idx3 = np.random.permutation(C)[:C]
    idx4 = np.random.permutation(C)[:O]
    idx5 = np.random.permutation(T)[:O]
    idx6 = np.random.permutation(O)[:E]
    idx7 = np.random.permutation(O)[:E]
    fk = mx_kscale(K)
    fr = mx_kscale(R)
    xtp = pack_weight(n((K, T)) / fk[:, None], "e2m1")
    wp = pack_weight(n((K, R)) * 1 / np.sqrt(K) * fk[:, None] * fr, "e4m3")
    wbp = pack_weight(n((R, N)) * 1 / np.sqrt(R) / fr[:, None], "e2m1")
    wsp = pack_weight(n((K, N)) * 1 / np.sqrt(K) * fk[:, None], "e4m3")
    return {
        "xt_words": xtp[0],
        "xt_scales": xtp[1],
        "w_words": wp[0],
        "w_scales": wp[1],
        "wb_words": wbp[0],
        "wb_scales": wbp[1],
        "ws_words": wsp[0],
        "ws_scales": wsp[1],
        "offs": striped(idx),
        "offs2": striped(idx2),
        "offs3": striped(idx3),
        "offs4": striped(idx4),
        "offs5": striped(idx5),
        "offs6": striped(idx6),
        "offs7": striped(idx7),
    }


def reference(xt_words, xt_scales, w_words, w_scales, wb_words, wb_scales, ws_words, ws_scales, offs, offs2, offs3, offs4, offs5, offs6, offs7):
    idx = unstriped(offs)
    idx2 = unstriped(offs2)
    idx3 = unstriped(offs3)
    idx4 = unstriped(offs4)
    idx5 = unstriped(offs5)
    idx6 = unstriped(offs6)
    idx7 = unstriped(offs7)
    xtu = unpack_weight(xt_words, xt_scales, "e2m1")
    wu = unpack_weight(w_words, w_scales, "e4m3")
    wbu = unpack_weight(wb_words, wb_scales, "e2m1")
    wsu = unpack_weight(ws_words, ws_scales, "e4m3")
    xtidxg = xtu[:, idx]
    a = wu.T @ xtidxg
    pw = np.zeros((R, C))
    pw[:, idx2] = a
    pg = np.maximum(pw, pw[:, idx3])
    hid = pg[:, idx4]
    hidq = mxq(hid, 0, "e5m2")
    xtidx5g = xtu[:, idx5]
    p = wbu.T @ hidq + wsu.T @ xtidx5g
    y = np.maximum(p[:, idx6], p[:, idx7])
    return y

@@ -1,0 +1,207 @@
+from contextlib import ExitStack
+
+import concourse.mybir as mybir
+
+K, T, J, R, C, O, N, E = 512, 1024, 256, 512, 512, 256, 256, 128
+FLOPS = 2 * K * R * J + 2 * R * N * O + 2 * K * N * O
+
+F32 = mybir.dt.float32
+BF16 = mybir.dt.bfloat16
+I32 = mybir.dt.int32
+U32 = mybir.dt.uint32
+U16 = mybir.dt.uint16
+U8 = mybir.dt.uint8
+E4M3 = mybir.dt.float8_e4m3fn_x4
+E5M2 = mybir.dt.float8_e5m2_x4
+E2M1 = mybir.dt.float4_e2m1fn_x4
+COPY = mybir.ActivationFunctionType.Copy
+MAX = mybir.AluOpType.max
+P = 128
+PACK = 4
+
+
+def tile_list_boardladder_solo_further_bestoftwo_kernel(
+    tc, xt_words, xt_scales, w_words, w_scales, wb_words, wb_scales, ws_words, ws_scales,
+    offs, offs2, offs3, offs4, offs5, offs6, offs7, out,
+):
+    nc = tc.nc
+
+    def move(on_vector, dst, src):
+        if on_vector:
+            nc.vector.tensor_copy(dst, src)
+        else:
+            nc.scalar.activation(dst, src, COPY)
+
+    with ExitStack() as ctx:
+        lists = ctx.enter_context(tc.tile_pool(name="lists", bufs=1))
+        sb = ctx.enter_context(tc.tile_pool(name="sb", bufs=1))
+        psum = ctx.enter_context(tc.psum_pool(name="psum", bufs=1))
+
+        def list_tile(name, n):
+            return lists.tile([P, n // 16], U16, name=name)
+
+        slot_token = list_tile("slot_token", J)
+        slot_column = list_tile("slot_column", J)
+        rival_column = list_tile("rival_column", C)
+        read_column = list_tile("read_column", O)
+        read_token = list_tile("read_token", O)
+        pair_first = list_tile("pair_first", E)
+        pair_second = list_tile("pair_second", E)
+
+        def tile(name, shape, dtype):
+            return sb.tile(shape, dtype, name=name, align_bytes=64)
+
+        xt_w = tile("xt_w", [P, T], U16)
+        xt_s = tile("xt_s", [P, T], U8)
+        w_w = tile("w_w", [P, R], U32)
+        w_s = tile("w_s", [P, R], U8)
+        wb_w = tile("wb_w", [P, N], U16)
+        wb_s = tile("wb_s", [P, N], U8)
+        ws_w = tile("ws_w", [P, N], U32)
+        ws_s = tile("ws_s", [P, N], U8)
+        board = [tile("board%d" % t, [P, C], F32) for t in range(PACK)]
+
+        def load_scales(queue, plane, rows, which):
+            for r in which:
+                queue.dma_start(plane[r:P:32, :].bitcast(I32), rows[0, r:16:4, :].bitcast(I32))
+
+        nc.vector.memset(xt_s[:].bitcast(I32), 0)
+        nc.vector.memset(w_s[:].bitcast(I32), 0)
+        nc.sync.dma_start(slot_token[:], offs)
+        nc.sync.dma_start(xt_w[:].bitcast(I32), xt_words[0].bitcast(I32))
+        load_scales(nc.scalar, xt_s, xt_scales, range(4))
+        nc.sync.dma_start(w_w[:].bitcast(I32), w_words[0].rearrange("p n t -> p (n t)").bitcast(I32))
+        load_scales(nc.sync, w_s, w_scales, range(4))
+        nc.vector.memset(ws_s[:].bitcast(I32), 0)
+        nc.vector.memset(wb_s[:].bitcast(I32), 0)
+        for t in range(PACK):
+            nc.vector.memset(board[t][:], 0.0)
+        nc.sync.dma_start(read_token[:], offs5)
+        nc.sync.dma_start(slot_column[:], offs2)
+        nc.sync.dma_start(rival_column[:], offs3)
+        nc.sync.dma_start(read_column[:], offs4)
+        nc.sync.dma_start(ws_w[:].bitcast(I32), ws_words[0].rearrange("p n t -> p (n t)").bitcast(I32))
+        load_scales(nc.sync, ws_s, ws_scales, range(4))
+        nc.sync.dma_start(wb_w[:].bitcast(I32), wb_words[0].bitcast(I32))
+        load_scales(nc.sync, wb_s, wb_scales, range(4))
+        nc.sync.dma_start(pair_first[:], offs6)
+        nc.sync.dma_start(pair_second[:], offs7)
+
+        w_wp = tile("w_wp", [P, R], U32)
+        w_sp = tile("w_sp", [P, R], U8)
+        xg_w = tile("xg_w", [P, J], U16)
+        xg_s = tile("xg_s", [P, J], U8)
+        xr_w = tile("xr_w", [P, O], U16)
+        xr_s = tile("xr_s", [P, O], U8)
+        nc.vector.tensor_copy(xg_s[:], xt_s[:].indirect(slot_token[:]))
+        nc.vector.tensor_copy(
+            w_wp[:].rearrange("p (t c i) -> p c t i", t=PACK, i=4),
+            w_w[:].rearrange("p (c i t) -> p c t i", t=PACK, i=4),
+        )
+        nc.vector.tensor_copy(xg_w[:], xt_w[:].indirect(slot_token[:]))
+        nc.vector.tensor_copy(
+            w_sp[:].rearrange("p (t c i) -> p c t i", t=PACK, i=16),
+            w_s[:].rearrange("p (c i t) -> p c t i", t=PACK, i=16),
+        )
+
+        a_ps = [psum.tile([P, J], F32, name="a_ps%d" % t) for t in range(PACK)]
+        for t in range(PACK):
+            cols = slice(P * t, P * (t + 1))
+            nc.tensor.matmul_mx(
+                out=a_ps[t][:], lhsT=w_wp[:, cols].bitcast(E4M3), lhsT_scale=w_sp[:, cols],
+                rhs=xg_w[:].bitcast(E2M1), rhs_scale=xg_s[:], start=True, stop=True,
+            )
+        nc.vector.tensor_copy(xr_w[:], xt_w[:].indirect(read_token[:]))
+        nc.vector.tensor_copy(xr_s[:], xt_s[:].indirect(read_token[:]))
+        p_ps = [psum.tile([P, O], F32, name="p_ps%d" % h) for h in range(2)]
+        for h in range(2):
+            cols = slice(P * h, P * (h + 1))
+            nc.tensor.matmul_mx(
+                out=p_ps[h][:], lhsT=ws_w[:, cols].bitcast(E4M3), lhsT_scale=ws_s[:, cols],
+                rhs=xr_w[:].bitcast(E2M1), rhs_scale=xr_s[:], start=True, stop=False,
+            )
+
+        a = [tile("a%d" % t, [P, J], F32) for t in range(PACK)]
+        rival = [tile("rival%d" % t, [P, C], F32) for t in range(PACK)]
+        kept = [tile("kept%d" % t, [P, C], F32) for t in range(PACK)]
+        hid = tile("hid", [P, O, PACK], BF16)
+        picked = tile("picked", [P, PACK, O], F32)
+
+        def empty(t, v):
+            if v:
+                nc.vector.tensor_copy(a[t][:], a_ps[t][:])
+            else:
+                nc.scalar.copy(a[t][:], a_ps[t][:])
+
+        def put(t, v):
+            move(v, board[t][:].indirect(slot_column[:]), a[t][:])
+
+        def look(t, half, v):
+            move(v, rival[t][:, 256 * half : 256 * (half + 1)], board[t][:].indirect(rival_column[:, 16 * half : 16 * (half + 1)]))
+
+        def keep(t):
+            nc.vector.tensor_tensor(kept[t][:], board[t][:], rival[t][:], MAX)
+
+        def read(t, v):
+            move(v, picked[:, t, :], kept[t][:].indirect(read_column[:]))
+
+        def read_half(t, half, v):
+            move(v, picked[:, t, 128 * half : 128 * (half + 1)], kept[t][:].indirect(read_column[:, 8 * half : 8 * (half + 1)]))
+
+        def read_step(t):
+            nc.vector.tensor_copy(hid[:, :, t], kept[t][:].indirect(read_column[:]))
+
+        empty(0, False)
+        put(0, False)
+        empty(1, True)
+        put(1, True)
+        empty(2, False)
+        put(2, False)
+        empty(3, True)
+        put(3, True)
+        for t in (0, 1):
+            look(t, 0, False)
+            look(t, 1, False)
+        look(3, 0, True)
+        look(3, 1, True)
+        look(2, 0, False)
+        look(2, 1, False)
+        keep(0)
+        keep(3)
+        keep(1)
+        read(0, False)
+        keep(2)
+        read(3, False)
+        read(1, True)
+        read_half(2, 0, True)
+        read_half(2, 1, False)
+        nc.vector.tensor_copy(
+            hid[:, 0:160, :].rearrange("p (c i) t -> p c t i", i=4),
+            picked[:, :, 0:160].rearrange("p t (c i) -> p c t i", i=4),
+        )
+        nc.scalar.copy(
+            hid[:, 160:256, :].rearrange("p (c i) t -> p c t i", i=4),
+            picked[:, :, 160:256].rearrange("p t (c i) -> p c t i", i=4),
+        )
+
+        hid_w = tile("hid_w", [P, O], U32)
+        hid_s = tile("hid_s", [P, O], U8)
+        nc.vector.quantize_mx(out=hid_w[:].bitcast(E5M2), scales=hid_s[:], in_=hid[:].rearrange("p o t -> p (o t)"))
+        for h in range(2):
+            cols = slice(P * h, P * (h + 1))
+            nc.tensor.matmul_mx(
+                out=p_ps[h][:], lhsT=wb_w[:, cols].bitcast(E2M1), lhsT_scale=wb_s[:, cols],
+                rhs=hid_w[:].bitcast(E5M2), rhs_scale=hid_s[:], start=False, stop=True,
+            )
+        p_sb = [tile("p_sb%d" % h, [P, O], F32) for h in range(2)]
+        first = [tile("first%d" % h, [P, E], F32) for h in range(2)]
+        second = [tile("second%d" % h, [P, E], F32) for h in range(2)]
+        y = [tile("y%d" % h, [P, E], F32) for h in range(2)]
+        nc.vector.tensor_copy(p_sb[0][:], p_ps[0][:])
+        nc.scalar.copy(p_sb[1][:], p_ps[1][:])
+        for h in range(2):
+            move(h == 0, first[h][:], p_sb[h][:].indirect(pair_first[:]))
+            move(h == 0, second[h][:], p_sb[h][:].indirect(pair_second[:]))
+        for h in range(2):
+            nc.vector.tensor_tensor(y[h][:], first[h][:], second[h][:], MAX)
+            (nc.sync if h == 0 else nc.scalar).dma_start(out[P * h : P * (h + 1), :], y[h][:])

@@ -18,6 +18,7 @@ COPY = mybir.ActivationFunctionType.Copy
 MAX = mybir.AluOpType.max
 P = 128
 PACK = 4
+BOARD = 544
 
 
 def tile_list_boardladder_solo_further_bestoftwo_kernel(
@@ -59,18 +60,19 @@ def tile_list_boardladder_solo_further_bestoftwo_kernel(
         wb_s = tile("wb_s", [P, N], U8)
         ws_w = tile("ws_w", [P, N], U32)
         ws_s = tile("ws_s", [P, N], U8)
-        board = [tile("board%d" % t, [P, C], F32) for t in range(PACK)]
+        board = [tile("board%d" % t, [P, BOARD], F32) for t in range(PACK)]
 
         def load_scales(queue, plane, rows, which):
             for r in which:
                 queue.dma_start(plane[r:P:32, :].bitcast(I32), rows[0, r:16:4, :].bitcast(I32))
 
-        nc.vector.memset(xt_s[:].bitcast(I32), 0)
+        nc.gpsimd.memset(xt_s[:].bitcast(I32), 0)
         nc.vector.memset(w_s[:].bitcast(I32), 0)
         nc.sync.dma_start(slot_token[:], offs)
+        load_scales(nc.sync, xt_s, xt_scales, range(3))
         nc.sync.dma_start(xt_w[:].bitcast(I32), xt_words[0].bitcast(I32))
-        load_scales(nc.scalar, xt_s, xt_scales, range(4))
         nc.sync.dma_start(w_w[:].bitcast(I32), w_words[0].rearrange("p n t -> p (n t)").bitcast(I32))
+        load_scales(nc.sync, xt_s, xt_scales, range(3, 4))
         load_scales(nc.sync, w_s, w_scales, range(4))
         nc.vector.memset(ws_s[:].bitcast(I32), 0)
         nc.vector.memset(wb_s[:].bitcast(I32), 0)
@@ -88,43 +90,51 @@ def tile_list_boardladder_solo_further_bestoftwo_kernel(
         nc.sync.dma_start(pair_second[:], offs7)
 
         w_wp = tile("w_wp", [P, R], U32)
-        w_sp = tile("w_sp", [P, R], U8)
+        w_sp0 = tile("w_sp0", [P, P], U8)
+        w_sp1 = tile("w_sp1", [P, R - P], U8)
+        w_sp = [w_sp0[:]] + [w_sp1[:, P * t : P * (t + 1)] for t in range(PACK - 1)]
         xg_w = tile("xg_w", [P, J], U16)
         xg_s = tile("xg_s", [P, J], U8)
         xr_w = tile("xr_w", [P, O], U16)
         xr_s = tile("xr_s", [P, O], U8)
         nc.vector.tensor_copy(xg_s[:], xt_s[:].indirect(slot_token[:]))
-        nc.vector.tensor_copy(
+        nc.scalar.copy(
             w_wp[:].rearrange("p (t c i) -> p c t i", t=PACK, i=4),
             w_w[:].rearrange("p (c i t) -> p c t i", t=PACK, i=4),
         )
         nc.vector.tensor_copy(xg_w[:], xt_w[:].indirect(slot_token[:]))
-        nc.vector.tensor_copy(
-            w_sp[:].rearrange("p (t c i) -> p c t i", t=PACK, i=16),
-            w_s[:].rearrange("p (c i t) -> p c t i", t=PACK, i=16),
-        )
+        w_s_dealt = w_s[:].rearrange("p (c i t) -> p c t i", t=PACK, i=16)
+        nc.vector.tensor_copy(w_sp0[:].rearrange("p (c i) -> p c i", i=16), w_s_dealt[:, :, 0, :])
+        nc.vector.tensor_copy(w_sp1[:].rearrange("p (t c i) -> p c t i", t=PACK - 1, i=16), w_s_dealt[:, :, 1:PACK, :])
 
         a_ps = [psum.tile([P, J], F32, name="a_ps%d" % t) for t in range(PACK)]
         for t in range(PACK):
             cols = slice(P * t, P * (t + 1))
             nc.tensor.matmul_mx(
-                out=a_ps[t][:], lhsT=w_wp[:, cols].bitcast(E4M3), lhsT_scale=w_sp[:, cols],
+                out=a_ps[t][:], lhsT=w_wp[:, cols].bitcast(E4M3), lhsT_scale=w_sp[t],
                 rhs=xg_w[:].bitcast(E2M1), rhs_scale=xg_s[:], start=True, stop=True,
             )
-        nc.vector.tensor_copy(xr_w[:], xt_w[:].indirect(read_token[:]))
-        nc.vector.tensor_copy(xr_s[:], xt_s[:].indirect(read_token[:]))
-        p_ps = [psum.tile([P, O], F32, name="p_ps%d" % h) for h in range(2)]
-        for h in range(2):
-            cols = slice(P * h, P * (h + 1))
-            nc.tensor.matmul_mx(
-                out=p_ps[h][:], lhsT=ws_w[:, cols].bitcast(E4M3), lhsT_scale=ws_s[:, cols],
-                rhs=xr_w[:].bitcast(E2M1), rhs_scale=xr_s[:], start=True, stop=False,
-            )
+        p_ps = [[psum.tile([P, O // 2], F32, name="p_ps%d%d" % (h, u)) for u in range(2)] for h in range(2)]
+
+        def short_words():
+            nc.vector.tensor_copy(xr_w[:], xt_w[:].indirect(read_token[:]))
+
+        def short_scales():
+            nc.vector.tensor_copy(xr_s[:], xt_s[:].indirect(read_token[:]))
+
+        def short_way():
+            for h in range(2):
+                cols = slice(P * h, P * (h + 1))
+                for u in range(2):
+                    reads = slice(128 * u, 128 * (u + 1))
+                    nc.tensor.matmul_mx(
+                        out=p_ps[h][u][:], lhsT=ws_w[:, cols].bitcast(E4M3), lhsT_scale=ws_s[:, cols],
+                        rhs=xr_w[:, reads].bitcast(E2M1), rhs_scale=xr_s[:, reads], start=True, stop=False,
+                    )
 
         a = [tile("a%d" % t, [P, J], F32) for t in range(PACK)]
         rival = [tile("rival%d" % t, [P, C], F32) for t in range(PACK)]
         kept = [tile("kept%d" % t, [P, C], F32) for t in range(PACK)]
-        hid = tile("hid", [P, O, PACK], BF16)
         picked = tile("picked", [P, PACK, O], F32)
 
         def empty(t, v):
@@ -139,8 +149,11 @@ def tile_list_boardladder_solo_further_bestoftwo_kernel(
         def look(t, half, v):
             move(v, rival[t][:, 256 * half : 256 * (half + 1)], board[t][:].indirect(rival_column[:, 16 * half : 16 * (half + 1)]))
 
+        def look_all(t):
+            nc.scalar.activation(rival[t][:], board[t][:].indirect(rival_column[:]), COPY)
+
         def keep(t):
-            nc.vector.tensor_tensor(kept[t][:], board[t][:], rival[t][:], MAX)
+            nc.vector.tensor_tensor(kept[t][:], board[t][:, 0:C], rival[t][:], MAX)
 
         def read(t, v):
             move(v, picked[:, t, :], kept[t][:].indirect(read_column[:]))
@@ -148,60 +161,63 @@ def tile_list_boardladder_solo_further_bestoftwo_kernel(
         def read_half(t, half, v):
             move(v, picked[:, t, 128 * half : 128 * (half + 1)], kept[t][:].indirect(read_column[:, 8 * half : 8 * (half + 1)]))
 
-        def read_step(t):
-            nc.vector.tensor_copy(hid[:, :, t], kept[t][:].indirect(read_column[:]))
-
+        short_words()
         empty(0, False)
-        put(0, False)
-        empty(1, True)
-        put(1, True)
-        empty(2, False)
-        put(2, False)
+        empty(1, False)
+        short_scales()
+        short_way()
+        empty(2, True)
         empty(3, True)
+        put(0, False)
+        put(1, False)
+        put(2, True)
         put(3, True)
-        for t in (0, 1):
-            look(t, 0, False)
-            look(t, 1, False)
-        look(3, 0, True)
-        look(3, 1, True)
-        look(2, 0, False)
-        look(2, 1, False)
+        look_all(0)
+        look_all(1)
+        look(2, 0, True)
+        look(2, 1, True)
+        look_all(3)
         keep(0)
-        keep(3)
-        keep(1)
-        read(0, False)
         keep(2)
-        read(3, False)
-        read(1, True)
-        read_half(2, 0, True)
-        read_half(2, 1, False)
-        nc.vector.tensor_copy(
-            hid[:, 0:160, :].rearrange("p (c i) t -> p c t i", i=4),
-            picked[:, :, 0:160].rearrange("p t (c i) -> p c t i", i=4),
-        )
-        nc.scalar.copy(
-            hid[:, 160:256, :].rearrange("p (c i) t -> p c t i", i=4),
-            picked[:, :, 160:256].rearrange("p t (c i) -> p c t i", i=4),
-        )
-
+        keep(1)
+        read(0, True)
+        keep(3)
+        read(2, False)
+        read(1, False)
+        read_half(3, 0, True)
+        read_half(3, 1, False)
         hid_w = tile("hid_w", [P, O], U32)
         hid_s = tile("hid_s", [P, O], U8)
-        nc.vector.quantize_mx(out=hid_w[:].bitcast(E5M2), scales=hid_s[:], in_=hid[:].rearrange("p o t -> p (o t)"))
-        for h in range(2):
-            cols = slice(P * h, P * (h + 1))
-            nc.tensor.matmul_mx(
-                out=p_ps[h][:], lhsT=wb_w[:, cols].bitcast(E2M1), lhsT_scale=wb_s[:, cols],
-                rhs=hid_w[:].bitcast(E5M2), rhs_scale=hid_s[:], start=False, stop=True,
-            )
+        half_hid = [tile("hid%d" % u, [P, O // 2, PACK], BF16) for u in range(2)]
+        for u in range(2):
+            cols = slice(128 * u, 128 * (u + 1))
+            dst = half_hid[u][:].rearrange("p (c i) t -> p c t i", i=4)
+            src = picked[:, :, cols].rearrange("p t (c i) -> p c t i", i=4)
+            if u == 0:
+                nc.vector.tensor_copy(dst, src)
+            else:
+                nc.scalar.copy(dst, src)
+        for u in range(2):
+            cols = slice(128 * u, 128 * (u + 1))
+            nc.vector.quantize_mx(out=hid_w[:, cols].bitcast(E5M2), scales=hid_s[:, cols], in_=half_hid[u][:].rearrange("p o t -> p (o t)"))
+            for h in range(2):
+                rows = slice(P * h, P * (h + 1))
+                nc.tensor.matmul_mx(
+                    out=p_ps[h][u][:], lhsT=wb_w[:, rows].bitcast(E2M1), lhsT_scale=wb_s[:, rows],
+                    rhs=hid_w[:, cols].bitcast(E5M2), rhs_scale=hid_s[:, cols], start=False, stop=True,
+                )
+
         p_sb = [tile("p_sb%d" % h, [P, O], F32) for h in range(2)]
         first = [tile("first%d" % h, [P, E], F32) for h in range(2)]
         second = [tile("second%d" % h, [P, E], F32) for h in range(2)]
         y = [tile("y%d" % h, [P, E], F32) for h in range(2)]
-        nc.vector.tensor_copy(p_sb[0][:], p_ps[0][:])
-        nc.scalar.copy(p_sb[1][:], p_ps[1][:])
+        for u in range(2):
+            cols = slice(128 * u, 128 * (u + 1))
+            nc.scalar.copy(p_sb[0][:, cols], p_ps[0][u][:])
+            nc.vector.tensor_copy(p_sb[1][:, cols], p_ps[1][u][:])
         for h in range(2):
-            move(h == 0, first[h][:], p_sb[h][:].indirect(pair_first[:]))
-            move(h == 0, second[h][:], p_sb[h][:].indirect(pair_second[:]))
+            move(h == 1, first[h][:], p_sb[h][:].indirect(pair_first[:]))
+            move(h == 1, second[h][:], p_sb[h][:].indirect(pair_second[:]))
         for h in range(2):
             nc.vector.tensor_tensor(y[h][:], first[h][:], second[h][:], MAX)
             (nc.sync if h == 0 else nc.scalar).dma_start(out[P * h : P * (h + 1), :], y[h][:])

@@ -66,20 +66,19 @@ def tile_list_boardladder_solo_further_bestoftwo_kernel(
             for r in which:
                 queue.dma_start(plane[r:P:32, :].bitcast(I32), rows[0, r:16:4, :].bitcast(I32))
 
-        nc.gpsimd.memset(xt_s[:].bitcast(I32), 0)
+        nc.vector.memset(xt_s[:].bitcast(I32), 0)
         nc.vector.memset(w_s[:].bitcast(I32), 0)
         nc.sync.dma_start(slot_token[:], offs)
-        load_scales(nc.sync, xt_s, xt_scales, range(3))
         nc.sync.dma_start(xt_w[:].bitcast(I32), xt_words[0].bitcast(I32))
+        nc.sync.dma_start(slot_column[:], offs2)
+        load_scales(nc.sync, xt_s, xt_scales, range(4))
         nc.sync.dma_start(w_w[:].bitcast(I32), w_words[0].rearrange("p n t -> p (n t)").bitcast(I32))
-        load_scales(nc.sync, xt_s, xt_scales, range(3, 4))
         load_scales(nc.sync, w_s, w_scales, range(4))
         nc.vector.memset(ws_s[:].bitcast(I32), 0)
         nc.vector.memset(wb_s[:].bitcast(I32), 0)
         for t in range(PACK):
             nc.vector.memset(board[t][:], 0.0)
         nc.sync.dma_start(read_token[:], offs5)
-        nc.sync.dma_start(slot_column[:], offs2)
         nc.sync.dma_start(rival_column[:], offs3)
         nc.sync.dma_start(read_column[:], offs4)
         nc.sync.dma_start(ws_w[:].bitcast(I32), ws_words[0].rearrange("p n t -> p (n t)").bitcast(I32))
@@ -97,12 +96,12 @@ def tile_list_boardladder_solo_further_bestoftwo_kernel(
         xg_s = tile("xg_s", [P, J], U8)
         xr_w = tile("xr_w", [P, O], U16)
         xr_s = tile("xr_s", [P, O], U8)
-        nc.vector.tensor_copy(xg_s[:], xt_s[:].indirect(slot_token[:]))
+        nc.vector.tensor_copy(xg_w[:], xt_w[:].indirect(slot_token[:]))
         nc.scalar.copy(
             w_wp[:].rearrange("p (t c i) -> p c t i", t=PACK, i=4),
             w_w[:].rearrange("p (c i t) -> p c t i", t=PACK, i=4),
         )
-        nc.vector.tensor_copy(xg_w[:], xt_w[:].indirect(slot_token[:]))
+        nc.vector.tensor_copy(xg_s[:], xt_s[:].indirect(slot_token[:]))
         w_s_dealt = w_s[:].rearrange("p (c i t) -> p c t i", t=PACK, i=16)
         nc.vector.tensor_copy(w_sp0[:].rearrange("p (c i) -> p c i", i=16), w_s_dealt[:, :, 0, :])
         nc.vector.tensor_copy(w_sp1[:].rearrange("p (t c i) -> p c t i", t=PACK - 1, i=16), w_s_dealt[:, :, 1:PACK, :])

@@ -70,7 +70,6 @@ def tile_list_boardladder_solo_further_bestoftwo_kernel(
         nc.vector.memset(w_s[:].bitcast(I32), 0)
         nc.sync.dma_start(slot_token[:], offs)
         nc.sync.dma_start(xt_w[:].bitcast(I32), xt_words[0].bitcast(I32))
-        nc.sync.dma_start(slot_column[:], offs2)
         load_scales(nc.sync, xt_s, xt_scales, range(4))
         nc.sync.dma_start(w_w[:].bitcast(I32), w_words[0].rearrange("p n t -> p (n t)").bitcast(I32))
         load_scales(nc.sync, w_s, w_scales, range(4))
@@ -79,6 +78,7 @@ def tile_list_boardladder_solo_further_bestoftwo_kernel(
         for t in range(PACK):
             nc.vector.memset(board[t][:], 0.0)
         nc.sync.dma_start(read_token[:], offs5)
+        nc.sync.dma_start(slot_column[:], offs2)
         nc.sync.dma_start(rival_column[:], offs3)
         nc.sync.dma_start(read_column[:], offs4)
         nc.sync.dma_start(ws_w[:].bitcast(I32), ws_words[0].rearrange("p n t -> p (n t)").bitcast(I32))
@@ -165,26 +165,29 @@ def tile_list_boardladder_solo_further_bestoftwo_kernel(
         empty(1, False)
         short_scales()
         short_way()
-        empty(2, True)
         empty(3, True)
+        empty(2, True)
         put(0, False)
         put(1, False)
-        put(2, True)
         put(3, True)
-        look_all(0)
-        look_all(1)
-        look(2, 0, True)
-        look(2, 1, True)
-        look_all(3)
+        put(2, False)
+        look(0, 0, True)
+        look(0, 1, True)
+        look(3, 0, True)
+        look(3, 1, True)
+        look_all(2)
         keep(0)
-        keep(2)
-        keep(1)
-        read(0, True)
         keep(3)
-        read(2, False)
-        read(1, False)
-        read_half(3, 0, True)
-        read_half(3, 1, False)
+        look(1, 0, True)
+        look(1, 1, False)
+        keep(2)
+        read(0, False)
+        keep(1)
+        read(3, False)
+        read_half(2, 0, True)
+        read_half(2, 1, False)
+        read_half(1, 0, True)
+        read_half(1, 1, False)
         hid_w = tile("hid_w", [P, O], U32)
         hid_s = tile("hid_s", [P, O], U8)
         half_hid = [tile("hid%d" % u, [P, O // 2, PACK], BF16) for u in range(2)]

from contextlib import ExitStack

import concourse.mybir as mybir

K, T, J, R, C, O, N, E = 512, 1024, 256, 512, 512, 256, 256, 128
FLOPS = 2 * K * R * J + 2 * R * N * O + 2 * K * N * O

F32 = mybir.dt.float32
BF16 = mybir.dt.bfloat16
I32 = mybir.dt.int32
U32 = mybir.dt.uint32
U16 = mybir.dt.uint16
U8 = mybir.dt.uint8
E4M3 = mybir.dt.float8_e4m3fn_x4
E5M2 = mybir.dt.float8_e5m2_x4
E2M1 = mybir.dt.float4_e2m1fn_x4
COPY = mybir.ActivationFunctionType.Copy
MAX = mybir.AluOpType.max
P = 128
PACK = 4
BOARD = 544


def tile_list_boardladder_solo_further_bestoftwo_kernel(
    tc, xt_words, xt_scales, w_words, w_scales, wb_words, wb_scales, ws_words, ws_scales,
    offs, offs2, offs3, offs4, offs5, offs6, offs7, out,
):
    nc = tc.nc

    def move(on_vector, dst, src):
        if on_vector:
            nc.vector.tensor_copy(dst, src)
        else:
            nc.scalar.activation(dst, src, COPY)

    with ExitStack() as ctx:
        lists = ctx.enter_context(tc.tile_pool(name="lists", bufs=1))
        sb = ctx.enter_context(tc.tile_pool(name="sb", bufs=1))
        psum = ctx.enter_context(tc.psum_pool(name="psum", bufs=1))

        def list_tile(name, n):
            return lists.tile([P, n // 16], U16, name=name)

        slot_token = list_tile("slot_token", J)
        slot_column = list_tile("slot_column", J)
        rival_column = list_tile("rival_column", C)
        read_column = list_tile("read_column", O)
        read_token = list_tile("read_token", O)
        pair_first = list_tile("pair_first", E)
        pair_second = list_tile("pair_second", E)

        def tile(name, shape, dtype):
            return sb.tile(shape, dtype, name=name, align_bytes=64)

        xt_w = tile("xt_w", [P, T], U16)
        xt_s = tile("xt_s", [P, T], U8)
        w_w = tile("w_w", [P, R], U32)
        w_s = tile("w_s", [P, R], U8)
        wb_w = tile("wb_w", [P, N], U16)
        wb_s = tile("wb_s", [P, N], U8)
        ws_w = tile("ws_w", [P, N], U32)
        ws_s = tile("ws_s", [P, N], U8)
        board = [tile("board%d" % t, [P, BOARD], F32) for t in range(PACK)]

        def load_scales(queue, plane, rows, which):
            for r in which:
                queue.dma_start(plane[r:P:32, :].bitcast(I32), rows[0, r:16:4, :].bitcast(I32))

        nc.vector.memset(xt_s[:].bitcast(I32), 0)
        nc.vector.memset(w_s[:].bitcast(I32), 0)
        nc.sync.dma_start(slot_token[:], offs)
        nc.sync.dma_start(xt_w[:].bitcast(I32), xt_words[0].bitcast(I32))
        load_scales(nc.sync, xt_s, xt_scales, range(4))
        nc.sync.dma_start(w_w[:].bitcast(I32), w_words[0].rearrange("p n t -> p (n t)").bitcast(I32))
        load_scales(nc.sync, w_s, w_scales, range(4))
        nc.vector.memset(ws_s[:].bitcast(I32), 0)
        nc.vector.memset(wb_s[:].bitcast(I32), 0)
        for t in range(PACK):
            nc.vector.memset(board[t][:], 0.0)
        nc.sync.dma_start(read_token[:], offs5)
        nc.sync.dma_start(slot_column[:], offs2)
        nc.sync.dma_start(rival_column[:], offs3)
        nc.sync.dma_start(read_column[:], offs4)
        nc.sync.dma_start(ws_w[:].bitcast(I32), ws_words[0].rearrange("p n t -> p (n t)").bitcast(I32))
        load_scales(nc.sync, ws_s, ws_scales, range(4))
        nc.sync.dma_start(wb_w[:].bitcast(I32), wb_words[0].bitcast(I32))
        load_scales(nc.sync, wb_s, wb_scales, range(4))
        nc.sync.dma_start(pair_first[:], offs6)
        nc.sync.dma_start(pair_second[:], offs7)

        w_wp = tile("w_wp", [P, R], U32)
        w_sp0 = tile("w_sp0", [P, P], U8)
        w_sp1 = tile("w_sp1", [P, R - P], U8)
        w_sp = [w_sp0[:]] + [w_sp1[:, P * t : P * (t + 1)] for t in range(PACK - 1)]
        xg_w = tile("xg_w", [P, J], U16)
        xg_s = tile("xg_s", [P, J], U8)
        xr_w = tile("xr_w", [P, O], U16)
        xr_s = tile("xr_s", [P, O], U8)
        nc.vector.tensor_copy(xg_w[:], xt_w[:].indirect(slot_token[:]))
        nc.scalar.copy(
            w_wp[:].rearrange("p (t c i) -> p c t i", t=PACK, i=4),
            w_w[:].rearrange("p (c i t) -> p c t i", t=PACK, i=4),
        )
        nc.vector.tensor_copy(xg_s[:], xt_s[:].indirect(slot_token[:]))
        w_s_dealt = w_s[:].rearrange("p (c i t) -> p c t i", t=PACK, i=16)
        nc.vector.tensor_copy(w_sp0[:].rearrange("p (c i) -> p c i", i=16), w_s_dealt[:, :, 0, :])
        nc.vector.tensor_copy(w_sp1[:].rearrange("p (t c i) -> p c t i", t=PACK - 1, i=16), w_s_dealt[:, :, 1:PACK, :])

        a_ps = [psum.tile([P, J], F32, name="a_ps%d" % t) for t in range(PACK)]
        for t in range(PACK):
            cols = slice(P * t, P * (t + 1))
            nc.tensor.matmul_mx(
                out=a_ps[t][:], lhsT=w_wp[:, cols].bitcast(E4M3), lhsT_scale=w_sp[t],
                rhs=xg_w[:].bitcast(E2M1), rhs_scale=xg_s[:], start=True, stop=True,
            )
        p_ps = [[psum.tile([P, O // 2], F32, name="p_ps%d%d" % (h, u)) for u in range(2)] for h in range(2)]

        def short_words():
            nc.vector.tensor_copy(xr_w[:], xt_w[:].indirect(read_token[:]))

        def short_scales():
            nc.vector.tensor_copy(xr_s[:], xt_s[:].indirect(read_token[:]))

        def short_way():
            for h in range(2):
                cols = slice(P * h, P * (h + 1))
                for u in range(2):
                    reads = slice(128 * u, 128 * (u + 1))
                    nc.tensor.matmul_mx(
                        out=p_ps[h][u][:], lhsT=ws_w[:, cols].bitcast(E4M3), lhsT_scale=ws_s[:, cols],
                        rhs=xr_w[:, reads].bitcast(E2M1), rhs_scale=xr_s[:, reads], start=True, stop=False,
                    )

        a = [tile("a%d" % t, [P, J], F32) for t in range(PACK)]
        rival = [tile("rival%d" % t, [P, C], F32) for t in range(PACK)]
        kept = [tile("kept%d" % t, [P, C], F32) for t in range(PACK)]
        picked = tile("picked", [P, PACK, O], F32)

        def empty(t, v):
            if v:
                nc.vector.tensor_copy(a[t][:], a_ps[t][:])
            else:
                nc.scalar.copy(a[t][:], a_ps[t][:])

        def put(t, v):
            move(v, board[t][:].indirect(slot_column[:]), a[t][:])

        def look(t, half, v):
            move(v, rival[t][:, 256 * half : 256 * (half + 1)], board[t][:].indirect(rival_column[:, 16 * half : 16 * (half + 1)]))

        def look_all(t):
            nc.scalar.activation(rival[t][:], board[t][:].indirect(rival_column[:]), COPY)

        def keep(t):
            nc.vector.tensor_tensor(kept[t][:], board[t][:, 0:C], rival[t][:], MAX)

        def read(t, v):
            move(v, picked[:, t, :], kept[t][:].indirect(read_column[:]))

        def read_half(t, half, v):
            move(v, picked[:, t, 128 * half : 128 * (half + 1)], kept[t][:].indirect(read_column[:, 8 * half : 8 * (half + 1)]))

        short_words()
        empty(0, False)
        empty(1, False)
        short_scales()
        short_way()
        empty(3, True)
        empty(2, True)
        put(0, False)
        put(1, False)
        put(3, True)
        put(2, False)
        look(0, 0, True)
        look(0, 1, True)
        look(3, 0, True)
        look(3, 1, True)
        look_all(2)
        keep(0)
        keep(3)
        look(1, 0, True)
        look(1, 1, False)
        keep(2)
        read(0, False)
        keep(1)
        read(3, False)
        read_half(2, 0, True)
        read_half(2, 1, False)
        read_half(1, 0, True)
        read_half(1, 1, False)
        hid_w = tile("hid_w", [P, O], U32)
        hid_s = tile("hid_s", [P, O], U8)
        half_hid = [tile("hid%d" % u, [P, O // 2, PACK], BF16) for u in range(2)]
        for u in range(2):
            cols = slice(128 * u, 128 * (u + 1))
            dst = half_hid[u][:].rearrange("p (c i) t -> p c t i", i=4)
            src = picked[:, :, cols].rearrange("p t (c i) -> p c t i", i=4)
            if u == 0:
                nc.vector.tensor_copy(dst, src)
            else:
                nc.scalar.copy(dst, src)
        for u in range(2):
            cols = slice(128 * u, 128 * (u + 1))
            nc.vector.quantize_mx(out=hid_w[:, cols].bitcast(E5M2), scales=hid_s[:, cols], in_=half_hid[u][:].rearrange("p o t -> p (o t)"))
            for h in range(2):
                rows = slice(P * h, P * (h + 1))
                nc.tensor.matmul_mx(
                    out=p_ps[h][u][:], lhsT=wb_w[:, rows].bitcast(E2M1), lhsT_scale=wb_s[:, rows],
                    rhs=hid_w[:, cols].bitcast(E5M2), rhs_scale=hid_s[:, cols], start=False, stop=True,
                )

        p_sb = [tile("p_sb%d" % h, [P, O], F32) for h in range(2)]
        first = [tile("first%d" % h, [P, E], F32) for h in range(2)]
        second = [tile("second%d" % h, [P, E], F32) for h in range(2)]
        y = [tile("y%d" % h, [P, E], F32) for h in range(2)]
        for u in range(2):
            cols = slice(128 * u, 128 * (u + 1))
            nc.scalar.copy(p_sb[0][:, cols], p_ps[0][u][:])
            nc.vector.tensor_copy(p_sb[1][:, cols], p_ps[1][u][:])
        for h in range(2):
            move(h == 1, first[h][:], p_sb[h][:].indirect(pair_first[:]))
            move(h == 1, second[h][:], p_sb[h][:].indirect(pair_second[:]))
        for h in range(2):
            nc.vector.tensor_tensor(y[h][:], first[h][:], second[h][:], MAX)
            (nc.sync if h == 0 else nc.scalar).dma_start(out[P * h : P * (h + 1), :], y[h][:])
